import numpy as np, ml_dtypes
CORES = [6,15,38,47]
N = 4
import mx_ref
BF = ml_dtypes.bfloat16
def entries(a):
    return np.ascontiguousarray(a.T).reshape(-1)
def table(e):
    return np.ascontiguousarray(np.reshape(e, (-1, 16)).T).astype(np.int32)
def cut(t, i, w=512):
    return t[:, w * i:w * i + w]
def f(rng, *shape):
    return mx_ref.flush((rng.standard_normal(shape, dtype=np.float32) * np.exp2(rng.integers(-2, 3, shape[:-1] + (1,)))).astype(BF))
def wide(rng, *shape, cols=0):
    v = rng.standard_normal(shape, dtype=np.float32) * np.exp2(rng.integers(-12, 13, shape)).astype(np.float32)
    if cols: v *= np.repeat(np.exp2(rng.integers(-cols, cols + 1, shape[:-2] + (1, shape[-1] // 4))) * (rng.random(shape[:-2] + (1, shape[-1] // 4)) > 0.0625), 4, axis=-1).astype(np.float32)
    return mx_ref.flush(v.astype(BF))
PG, NW, SP, CW, CP, O = 32, 128, 32, 48, 12, 2
def counts(rng, total, cap, least):
    n = np.array(least)
    while n.sum() < total: n[rng.choice(np.flatnonzero(n < cap))] += 1
    return n
def lists(rng, full=False, own=False, shared=False, rewritten=False):
    h = int(rng.integers(0, N)); hot = rng.permutation(PG)[:CP if shared else 2]
    fr, pg = np.zeros((N, SP), int), np.zeros((N, SP), int)
    rd, wr, wp = np.full((N, N * CP), -1), np.full((N, N * CW), -1), np.full((N, N * CW), -1)
    for s in range(N):
        lw, lp = np.zeros(N, int), np.zeros(N, int)
        if full:
            a = np.append(h, rng.permutation(np.delete(np.arange(N), h)))
            lw[a[:NW // CW]] = CW; lp[a[:SP // CP]] = CP
        if own: lw[s] = CW; lp[s] = CP
        if shared: lw[h] = CW; lp[h] = CP
        if rewritten: lw[h] = CW; lp[h] = 1
        n, fresh, at = counts(rng, NW, CW, lw), rng.permutation(NW), 0
        for q in range(N):
            c = rng.permutation(CW)[:n[q]]
            wr[s, q * CW + c] = fresh[at:at + n[q]]; wp[q, s * CW + c] = 0; at += n[q]
        n, slots, frames = counts(rng, SP, CP, lp), [], []
        for q in range(N):
            must = np.zeros(0, int)
            if q == h and shared: must = hot
            if q == h and rewritten: must = hot[s % 2:s % 2 + 1]
            g = np.concatenate([must, rng.permutation(np.setdiff1d(np.arange(PG), must))])[:n[q]]
            c = rng.permutation(CP)[:n[q]]
            rd[q, s * CP + c] = g; slots.append(q * CP + c); frames.append(q * PG + g)
        o = rng.permutation(SP)
        pg[s] = np.concatenate(slots)[o]; fr[s] = np.concatenate(frames)[o]
    for q in range(N):
        k = np.flatnonzero(wp[q] >= 0); must = np.zeros(0, int)
        if q == h and shared: must = 16 * hot + rng.integers(0, 16, hot.size)
        if q == h and rewritten: must = (16 * hot[:, None] + np.arange(16)).reshape(-1)
        p = np.concatenate([must, rng.permutation(np.setdiff1d(np.arange(16 * PG), must))])[:k.size]
        wp[q, k] = rng.permutation(p)
    return {n: np.stack([table(v) for v in a]) for n, a in (("fr", fr), ("wr", wr), ("wp", wp), ("rd", rd), ("pg", pg))}
def setup_inputs(rng):
    return {"pl": f(rng, N, 128, 64 * PG), "nw": f(rng, N, 128, 4 * NW), "qw": f(rng, N, 128, 512 * O), **lists(rng)}
def setup_inputs_full(rng):
    return {**setup_inputs(rng), **lists(rng, full=True)}
def setup_inputs_own(rng):
    return {**setup_inputs(rng), **lists(rng, own=True)}
def setup_inputs_rewritten(rng):
    return {**setup_inputs(rng), **lists(rng, rewritten=True)}
def setup_inputs_shared(rng):
    return {**setup_inputs(rng), **lists(rng, shared=True)}
def setup_inputs_spread(rng):
    d = setup_inputs(rng); d["pl"] = wide(rng, N, 128, 64 * PG, cols=8); d["nw"] = wide(rng, N, 128, 4 * NW, cols=8); return d
def check_inputs(d):
    b = []
    for r in range(N):
        t, a, p, k, g = [entries(d[n][r]) for n in ("fr", "wr", "wp", "rd", "pg")]
        if t.min() < 0 or t.max() >= N * PG or len(set(t.tolist())) != SP: b.append("fr")
        if a.min() < -1 or a.max() >= NW or sorted(a[a >= 0].tolist()) != list(range(NW)): b.append("wr")
        sent = np.concatenate([entries(d["wr"][s])[r * CW:r * CW + CW] for s in range(N)]); v = p[p >= 0]
        if p.min() < -1 or p.max() >= 16 * PG or len(set(v.tolist())) != v.size or ((p >= 0) != (sent >= 0)).any(): b.append("wp")
        if k.min() < -1 or k.max() >= PG: b.append("rd")
        got = np.concatenate([entries(d["rd"][q])[r * CP:r * CP + CP] for q in range(N)])
        if g.min() < 0 or g.max() >= N * CP or len(set(g.tolist())) != SP or (got >= 0).sum() != SP: b.append("pg")
        elif (got[g] < 0).any() or (g // CP * PG + got[g] != t).any(): b.append("pg")
    return b
def reference(pl, nw, qw, fr, wr, wp, rd, pg):
    pools = []
    for q in range(N):
        v = pl[q].reshape(128, 16 * PG, 4).copy()
        for s in range(N):
            c, p = entries(wr[s])[q * CW:q * CW + CW], entries(wp[q])[s * CW:s * CW + CW]
            k = p >= 0
            v[:, p[k]] = nw[s].reshape(128, NW, 4)[:, c[k]]
        pools.append(v)
    pools = np.concatenate(pools, axis=1)
    y = np.zeros((N, 128, O * SP * 16), np.float32)
    for r in range(N):
        e = (16 * entries(fr[r])[:, None] + np.arange(16)).reshape(-1)
        pages = mx_ref.quantize(np.ascontiguousarray(pools[:, e]).reshape(128, -1))
        for o in range(O):
            y[r][:, SP * 16 * o:SP * 16 * o + SP * 16] = mx_ref.matmul(mx_ref.quantize(np.ascontiguousarray(cut(qw[r], o))), pages)
    return {"y": y}

@@ -1,0 +1,249 @@
+from concourse.bass import DstId, RemoteDMATransfer
+from concourse.mybir import dt, AluOpType, ActivationFunctionType
+
+N = 4
+PG, NW, SP, CW, CP, O = 32, 128, 32, 48, 12, 2
+POOL = 16 * PG
+WIN = POOL + N * CW
+PC = 16 * CP
+WT = POOL + 32
+WALL = WT + 16 + N * CW + 112 + 16
+X4 = WT // 4
+X = "float8_e4m3fn_x4"
+
+SCRATCH = {
+    "nwt": ("sbuf", [128, 4 * NW], "bfloat16"), "plt": ("sbuf", [128, 4 * POOL], "bfloat16"), "qwt": ("sbuf", [128, 512 * O], "bfloat16"),
+    "lwr": ("sbuf", [128, 12], "int32"), "lwp": ("sbuf", [128, 12], "int32"), "lrd": ("sbuf", [128, 3], "int32"), "lpg": ("sbuf", [128, 2], "int32"),
+    "nwc": ("sbuf", [128, NW], X), "nws": ("sbuf", [128, NW], "uint8"),
+    "ac": ("sbuf", [128, N * CW], X), "asc": ("sbuf", [128, N * CW], "uint8"),
+    "wc": ("sbuf", [128, WIN], X), "wsc": ("sbuf", [128, WIN], "uint8"),
+    "bc": ("sbuf", [128, N * PC], X), "bsc": ("sbuf", [128, N * PC], "uint8"),
+    "pc": ("sbuf", [128, N * PC], X), "psc": ("sbuf", [128, N * PC], "uint8"),
+    "qwc": ("sbuf", [128, 128 * O], X), "qws": ("sbuf", [128, 128 * O], "uint8"),
+    "part": ("sbuf", [128, 1], "int32"), "pi": ("sbuf", [128, 1], "int32"), "ph": ("sbuf", [128, 1], "int32"), "po": ("sbuf", [128, 1], "int32"),
+    "h16": ("sbuf", [128, 1], "float32"), "ca": ("sbuf", [128, 1], "float32"), "cb": ("sbuf", [128, 1], "float32"), "cc": ("sbuf", [128, 1], "float32"), "fi": ("sbuf", [128, 1], "float32"),
+    "xi": ("sbuf", [128, X4], "float32"), "val": ("sbuf", [128, N * CW], "float32"), "kt": ("sbuf", [128, 12], "int32"),
+    "clb": ("sbuf", [128, 2], "float32"), "s16": ("sbuf", [128, N * CP], "float32"), "cw": ("sbuf", [128, N * CP], "float32"),
+    "clo": ("sbuf", [128, 2], "uint16"), "wro": ("sbuf", [128, 12], "uint16"), "owno": ("sbuf", [128, 4], "uint16"),
+    "wpo": ("sbuf", [128, 12], "uint16"), "rdo": ("sbuf", [128, 4], "uint16"), "pgo": ("sbuf", [128, 2], "uint16"),
+    "boff": ("sbuf", [128, N * CP], "uint16"), "yoff": ("sbuf", [128, SP], "uint16"),
+    "ta": ("sbuf", [128, 12], "int32"), "tb": ("sbuf", [128, 12], "int32"), "tc": ("sbuf", [128, 12], "int32"),
+    "w": ("sbuf", [128, WALL], "float32"), "wt": ("sbuf", [128, WT], "float32"), "wm": ("sbuf", [128, PG], "float32"),
+    "r0": ("sbuf", [128, N * PC], "float32"), "r1": ("sbuf", [128, N * PC], "float32"),
+    "yt": ("sbuf", [128, 512 * O], "float32"),
+    "ps": ("psum", [128, 512 * 2 * N], "float32"),
+}
+TOK = 110
+SEMAPHORES = ["t%d" % i for i in range(TOK)] + ["ra%d" % i for i in range(N)] + ["rb%d" % i for i in range(N)] + ["left"]
+
+
+def rank_program(g, core, T, topo):
+    rank = T.rank_of(core)
+    if rank is None:
+        return
+    V, S, Y, PE = g.vector, g.scalar, g.sync, g.tensor
+    A, COPY = AluOpType, ActivationFunctionType.Copy
+    cores = list(T.cores)
+
+    used, seen, toks = [0], set(), []
+    queues = {"g": g, "v": V, "s": S, "y": Y, "t": PE}
+
+    def tok():
+        k = "t%d" % used[0]
+        used[0] += 1
+        return k
+
+    def done(ins, n=1):
+        k = tok()
+        ins.then_inc(T.sem[k], n)
+        toks.append((k, n))
+        return (k, n)
+
+    def wait(q, *ts):
+        for t in ts:
+            if (q, t) not in seen:
+                seen.add((q, t))
+                queues[q].wait_ge(T.sem[t[0]], t[1])
+
+    def hops(d):
+        a, b = topo.chip(core), topo.chip(cores[d])
+        return 0 if topo.mates(a, b) else 1 if topo.same_plane(a, b) else 2
+
+    others = sorted([d for d in range(N) if d != rank], key=lambda d: -hops(d))
+
+    def mask(d, a, b):
+        e = topo.engines(core, cores[d])
+        n = len(e)
+        return sum(1 << k for k in e[a * n // 8:b * n // 8])
+
+    def transfer(d, a, b, src, dst, sem):
+        rid, pid, _ = topo.addr(cores[d])
+        return RemoteDMATransfer(dst_ids=[DstId(rid=rid, pnc=pid)], dma_engine_mask=mask(d, a, b), remote_sem=T.sem[sem], src=src, dst=dst)
+
+    left = [0]
+
+    def engines_in(a, b):
+        n = len(topo.engines(core, cores[others[0]]))
+        return b * n // 8 - a * n // 8
+
+    def fused(parts, sem):
+        g.remote_dma_fused([transfer(d, a, b, s, t, sem) for d, a, b, s, t in parts], local_sem=T.sem.left)
+        left[0] += sum(engines_in(a, b) for d, a, b, s, t in parts)
+
+    def lists(dst, src, n, halves):
+        k = tok()
+        for q, gr in halves:
+            for i in gr:
+                queues[q].dma_start(dst[16 * i:16 * i + 16, 0:n], src[:]).then_inc(T.sem[k], 16)
+        toks.append((k, 128))
+        return (k, 128)
+
+    lo, hi = range(0, 4), range(4, 8)
+    l_nw = done(Y.dma_start(T.nwt[:], T.nw[:]), 16)
+    l_wr = lists(T.lwr, T.wr, 12, (("s", hi), ("y", lo)))
+    l_wp = lists(T.lwp, T.wp, 12, (("s", hi), ("y", lo)))
+    l_rd = lists(T.lrd, T.rd, 3, (("s", hi), ("y", lo)))
+    half = 2 * POOL
+    l_p0 = done(Y.dma_start(T.plt[:, 0:half], T.pl[:, 0:half]), 16)
+    l_p1 = done(S.dma_start(T.plt[:, half:2 * half], T.pl[:, half:2 * half]), 16)
+    l_qw = done(Y.dma_start(T.qwt[:], T.qw[:]), 16)
+    l_pg = lists(T.lpg, T.pg, 2, (("y", range(0, 8)),))
+
+    i_p = done(g.iota(T.part[:], [[1, 1]], 0, 1))
+    i_x = done(g.iota(T.xi[:], [[1, X4]], 0, 0, allow_small_or_imprecise_dtypes=True))
+    i_c = done(g.iota(T.clb[:], [[16 * 16, 2]], 0, 0, allow_small_or_imprecise_dtypes=True))
+    i_k = done(g.iota(T.kt[:], [[16, 12]], WT + 1, 1))
+    i_v = done(g.iota(T.val[:], [[1, N * CW]], POOL, 0, allow_small_or_imprecise_dtypes=True))
+
+    wait("v", i_p)
+    c_h = done(V.tensor_scalar(T.ph[:], T.part[:], 4, 1, A.logical_shift_right, A.bitwise_and))
+    c_i = done(V.tensor_scalar(T.pi[:], T.part[:], 15, None, A.bitwise_and))
+    c_o = done(V.tensor_scalar(T.po[:], T.part[:], 1, None, A.bitwise_and))
+    wait("v", c_h)
+    c_h16 = done(V.tensor_scalar(T.h16[:], T.ph[:], 16.0, None, A.mult))
+    c_a = done(V.tensor_scalar(T.ca[:], T.ph[:], -64.0, 32.0, A.mult, A.add))
+    wait("v", c_h16, i_x)
+    c_w = [done(V.tensor_scalar(T.w[:, X4 * k:X4 * k + X4], T.xi[:], float(X4 * k), T.h16[:], A.add, A.subtract)) for k in range(4)]
+    wait("v", c_o, c_a)
+    c_b = done(V.tensor_scalar(T.cb[:], T.po[:], T.ca[:], T.h16[:], A.mult, A.add))
+    wait("v", c_b, c_i)
+    c_c = done(V.tensor_scalar(T.cc[:], T.pi[:], 16.0, T.cb[:], A.mult, A.add))
+    c_f = done(V.tensor_copy(T.fi[:], T.pi[:]))
+    wait("v", c_c, i_c)
+    c_cl = done(V.tensor_scalar(T.clo[:], T.clb[:], T.cc[:], None, A.add))
+
+    wait("v", l_wr)
+    o_wr = done(V.tensor_scalar(T.wro[:], T.lwr[:], 0.0, None, A.max))
+    wait("v", l_nw)
+    q_nw = done(V.quantize_mx(T.nwc[:], T.nws[:], T.nwt[:]))
+    wait("v", o_wr, q_nw)
+    a_c = done(V.tensor_copy(T.ac[:].bitcast(dt.uint32), T.nwc[:].bitcast(dt.uint32).indirect(T.wro[:])))
+    wait("s", o_wr, q_nw)
+    a_s = done(S.activation(T.asc[:], T.nws[:].indirect(T.wro[:]), COPY))
+    o_own = done(V.tensor_scalar(T.owno[:, 0:3], T.lwr[:, 3 * rank:3 * rank + 3], 0.0, None, A.max))
+
+    wait("g", a_c, a_s)
+    at = POOL + CW * rank
+    share = [(0, 4), (4, 6), (6, 8)], [(4, 8), (0, 2), (2, 4)]
+    cut = lambda t, i, w: t[:, w * i:w * i + w]
+    fused([(d, a, b, cut(T.ac, d, CW).bitcast(dt.uint8), T.wc[:, at:at + CW].bitcast(dt.uint8)) for d, (a, b) in zip(others, share[0])], "ra%d" % rank)
+    fused([(d, a, b, cut(T.asc, d, CW), T.wsc[:, at:at + CW]) for d, (a, b) in zip(others, share[1])], "ra%d" % rank)
+    i_s = done(g.iota(T.s16[:], [[16, N * CP]], 0, 0, allow_small_or_imprecise_dtypes=True))
+
+    def a_count(s):
+        o = sorted([d for d in range(N) if d != s], key=lambda d: -(0 if topo.mates(topo.chip(cores[s]), topo.chip(cores[d])) else 1 if topo.same_plane(topo.chip(cores[s]), topo.chip(cores[d])) else 2))
+        k = o.index(rank)
+        return sum(engines_in(*sh[k]) for sh in share)
+
+    wait("v", l_wp)
+    b_1 = done(V.tensor_scalar(T.ta[:], T.lwp[:], 0.0, None, A.is_lt))
+    wait("v", i_k, b_1)
+    b_2 = done(V.tensor_tensor(T.tb[:], T.ta[:], T.kt[:], A.mult))
+    wait("v", b_2)
+    b_3 = done(V.tensor_tensor(T.tc[:], T.tb[:], T.lwp[:], A.add))
+    wait("v", b_3)
+    b_4 = done(V.tensor_scalar(T.wpo[:], T.tc[:], T.h16[:], None, A.add))
+    wait("v", l_rd)
+    b_5 = done(V.tensor_scalar(T.rdo[:, 0:3], T.lrd[:], 0.0, None, A.max))
+    wait("v", b_4, i_v, *c_w)
+    b_6 = done(V.tensor_copy(T.w[:].indirect(T.wpo[:]), T.val[:]))
+    wait("v", o_own)
+    n_c = done(V.tensor_copy(T.wc[:, at:at + CW].bitcast(dt.uint32), T.nwc[:].bitcast(dt.uint32).indirect(T.owno[:, 0:3])))
+    wait("s", o_own)
+    n_s = done(S.activation(T.wsc[:, at:at + CW], T.nws[:].indirect(T.owno[:, 0:3]), COPY))
+    wait("v", b_6)
+    b_7 = done(V.transpose(T.wt[:], T.w[:, 0:WT]))
+    wait("v", b_7, c_cl)
+    b_8 = done(V.tensor_copy(T.wm[:], T.wt[:].indirect(T.clo[:])))
+    wait("v", b_8, b_5)
+    b_9 = done(V.tensor_copy(T.boff[:], T.wm[:].indirect(T.rdo[:, 0:3])))
+    hp = POOL // 2
+    wait("v", l_p0)
+    q_p0 = done(V.quantize_mx(T.wc[:, 0:hp], T.wsc[:, 0:hp], T.plt[:, 0:half]))
+    wait("v", l_p1)
+    q_p1 = done(V.quantize_mx(T.wc[:, hp:POOL], T.wsc[:, hp:POOL], T.plt[:, half:2 * half]))
+    wait("v", l_qw)
+    q_qw = done(V.quantize_mx(T.qwc[:], T.qws[:], T.qwt[:]))
+
+    arrived = [("ra%d" % s, a_count(s)) for s in others]
+    b_c, b_s = {}, {}
+    for q in ("v", "s"):
+        wait(q, b_9, q_p0, q_p1, n_c, n_s, *arrived)
+    for d in others + [rank]:
+        c, s = (T.pc, T.psc) if d == rank else (T.bc, T.bsc)
+        b_c[d] = done(V.tensor_copy(cut(c, d, PC).bitcast(dt.uint32), T.wc[:].bitcast(dt.uint32).indirect(cut(T.boff, d, CP))))
+        b_s[d] = done(S.activation(cut(s, d, PC), T.wsc[:].indirect(cut(T.boff, d, CP)), COPY))
+    rb = "rb%d" % rank
+    codes = lambda d, a, b: (d, a, b, cut(T.bc, d, PC).bitcast(dt.uint8), cut(T.pc, rank, PC).bitcast(dt.uint8))
+    scales = lambda d, a, b: (d, a, b, cut(T.bsc, d, PC), cut(T.psc, rank, PC))
+    wait("g", b_c[others[0]])
+    fused([codes(others[0], 0, 8)], rb)
+    wait("g", b_c[others[1]])
+    fused([codes(others[1], 0, 8)], rb)
+    wait("g", b_s[others[0]], b_s[others[1]])
+    fused([scales(others[0], 0, 4), scales(others[1], 4, 8)], rb)
+    wait("g", b_c[others[2]])
+    fused([codes(others[2], 0, 8)], rb)
+    wait("g", b_s[others[2]])
+    fused([scales(others[2], 0, 8)], rb)
+
+    def b_count(s):
+        return engines_in(0, 8) + (engines_in(0, 8) if hops(s) == min(hops(d) for d in others) else engines_in(0, 4))
+
+    wait("v", l_pg, i_s, c_f)
+    y_1 = done(V.tensor_copy(T.pgo[:], T.lpg[:]))
+    y_2 = done(V.tensor_scalar(T.cw[:], T.s16[:], T.fi[:], None, A.add))
+    wait("v", y_1, y_2)
+    y_3 = done(V.tensor_copy(T.yoff[:], T.cw[:].indirect(T.pgo[:])))
+
+    got = []
+    for k, s in enumerate([rank] + others):
+        if s == rank:
+            wait("t", q_qw, b_c[s], b_s[s])
+        else:
+            wait("t", ("rb%d" % s, b_count(s)))
+        for o in range(O):
+            at = 512 * (O * k + o)
+            m = done(PE.matmul_mx(T.ps[:, at:at + PC], cut(T.qwc, o, 128), cut(T.qws, o, 128), cut(T.pc, s, PC), cut(T.psc, s, PC), True, True))
+            if o == 0:
+                wait("v", m)
+                got.append(done(V.tensor_copy(cut(T.r0, s, PC), T.ps[:, at:at + PC])))
+            else:
+                wait("s", m)
+                got.append(done(S.activation(cut(T.r1, s, PC), T.ps[:, at:at + PC], COPY)))
+
+    wait("v", y_3, *got[0::2])
+    wait("s", y_3, *got[1::2])
+    for k in range(2):
+        a, b = 256 * k, 256 * k + 256
+        f0 = done(V.tensor_copy(T.yt[:, a:b], T.r0[:].indirect(T.yoff[:, a // 16:b // 16])))
+        f1 = done(S.activation(T.yt[:, 512 + a:512 + b], T.r1[:].indirect(T.yoff[:, a // 16:b // 16]), COPY))
+        wait("y", f0)
+        done(Y.dma_start(T.y[:, a:b], T.yt[:, a:b]), 16)
+        wait("y", f1)
+        done(Y.dma_start(T.y[:, 512 + a:512 + b], T.yt[:, 512 + a:512 + b]), 16)
+
+    for t in toks:
+        if not any((q, t) in seen for q in queues):
+            wait("y", t)
+    g.wait_ge(T.sem.left, left[0])

@@ -9,13 +9,14 @@ PC = 16 * CP
 WT = POOL + 32
 WALL = WT + 16 + N * CW + 112 + 16
 X4 = WT // 4
+AW = 64
 X = "float8_e4m3fn_x4"
 
 SCRATCH = {
     "nwt": ("sbuf", [128, 4 * NW], "bfloat16"), "plt": ("sbuf", [128, 4 * POOL], "bfloat16"), "qwt": ("sbuf", [128, 512 * O], "bfloat16"),
     "lwr": ("sbuf", [128, 12], "int32"), "lwp": ("sbuf", [128, 12], "int32"), "lrd": ("sbuf", [128, 3], "int32"), "lpg": ("sbuf", [128, 2], "int32"),
     "nwc": ("sbuf", [128, NW], X), "nws": ("sbuf", [128, NW], "uint8"),
-    "ac": ("sbuf", [128, N * CW], X), "asc": ("sbuf", [128, N * CW], "uint8"),
+    "ac": ("sbuf", [128, N * AW], X), "asc": ("sbuf", [128, N * AW], "uint8"),
     "wc": ("sbuf", [128, WIN], X), "wsc": ("sbuf", [128, WIN], "uint8"),
     "bc": ("sbuf", [128, N * PC], X), "bsc": ("sbuf", [128, N * PC], "uint8"),
     "pc": ("sbuf", [128, N * PC], X), "psc": ("sbuf", [128, N * PC], "uint8"),
@@ -27,14 +28,18 @@ SCRATCH = {
     "clo": ("sbuf", [128, 2], "uint16"), "wro": ("sbuf", [128, 12], "uint16"), "owno": ("sbuf", [128, 4], "uint16"),
     "wpo": ("sbuf", [128, 12], "uint16"), "rdo": ("sbuf", [128, 4], "uint16"), "pgo": ("sbuf", [128, 2], "uint16"),
     "boff": ("sbuf", [128, N * CP], "uint16"), "yoff": ("sbuf", [128, SP], "uint16"),
-    "ta": ("sbuf", [128, 12], "int32"), "tb": ("sbuf", [128, 12], "int32"), "tc": ("sbuf", [128, 12], "int32"),
+    "ta": ("sbuf", [128, 12], "int32"), "tb": ("sbuf", [128, 12], "int32"),
     "w": ("sbuf", [128, WALL], "float32"), "wt": ("sbuf", [128, WT], "float32"), "wm": ("sbuf", [128, PG], "float32"),
     "r0": ("sbuf", [128, N * PC], "float32"), "r1": ("sbuf", [128, N * PC], "float32"),
     "yt": ("sbuf", [128, 512 * O], "float32"),
     "ps": ("psum", [128, 512 * 2 * N], "float32"),
 }
 TOK = 110
-SEMAPHORES = ["t%d" % i for i in range(TOK)] + ["ra%d" % i for i in range(N)] + ["rb%d" % i for i in range(N)] + ["left"]
+SEMAPHORES = ["t%d" % i for i in range(TOK)] + [p + "%d" % i for p in ("ra", "sa", "rb") for i in range(N)] + ["left"]
+
+A_CALLS = [("c", [(0, 0, 4)]), ("c", [(1, 4, 6), (2, 6, 8)]), ("s", [(0, 4, 8), (1, 0, 2), (2, 2, 4)])]
+B_CALLS = [("c", [(0, 0, 8)]), ("c", [(1, 0, 8)]), ("s", [(0, 0, 4), (1, 4, 8)]), ("c", [(2, 0, 8)]), ("s", [(2, 0, 8)])]
+PIECES = [(0, 192), (192, 512)]
 
 
 def rank_program(g, core, T, topo):
@@ -65,30 +70,33 @@ def rank_program(g, core, T, topo):
                 seen.add((q, t))
                 queues[q].wait_ge(T.sem[t[0]], t[1])
 
-    def hops(d):
-        a, b = topo.chip(core), topo.chip(cores[d])
+    def hops(s, d):
+        a, b = topo.chip(cores[s]), topo.chip(cores[d])
         return 0 if topo.mates(a, b) else 1 if topo.same_plane(a, b) else 2
 
-    others = sorted([d for d in range(N) if d != rank], key=lambda d: -hops(d))
+    def away(s):
+        return sorted([d for d in range(N) if d != s], key=lambda d: -hops(s, d))
 
-    def mask(d, a, b):
+    others = away(rank)
+
+    def engines(d, a, b):
         e = topo.engines(core, cores[d])
-        n = len(e)
-        return sum(1 << k for k in e[a * n // 8:b * n // 8])
-
-    def transfer(d, a, b, src, dst, sem):
-        rid, pid, _ = topo.addr(cores[d])
-        return RemoteDMATransfer(dst_ids=[DstId(rid=rid, pnc=pid)], dma_engine_mask=mask(d, a, b), remote_sem=T.sem[sem], src=src, dst=dst)
+        return e[a * len(e) // 8:b * len(e) // 8]
 
     left = [0]
 
-    def engines_in(a, b):
-        n = len(topo.engines(core, cores[others[0]]))
-        return b * n // 8 - a * n // 8
-
     def fused(parts, sem):
-        g.remote_dma_fused([transfer(d, a, b, s, t, sem) for d, a, b, s, t in parts], local_sem=T.sem.left)
-        left[0] += sum(engines_in(a, b) for d, a, b, s, t in parts)
+        ts = []
+        for d, a, b, src, dst in parts:
+            rid, pid, _ = topo.addr(cores[d])
+            e = engines(d, a, b)
+            ts.append(RemoteDMATransfer(dst_ids=[DstId(rid=rid, pnc=pid)], dma_engine_mask=sum(1 << k for k in e), remote_sem=T.sem[sem], src=src, dst=dst))
+            left[0] += len(e)
+        g.remote_dma_fused(ts, local_sem=T.sem.left)
+
+    def count(calls, s, kinds):
+        n = len(topo.engines(cores[s], core))
+        return sum(b * n // 8 - a * n // 8 for kind, parts in calls for k, a, b in parts if kind in kinds and away(s)[k] == rank)
 
     def lists(dst, src, n, halves):
         k = tok()
@@ -99,20 +107,19 @@ def rank_program(g, core, T, topo):
         return (k, 128)
 
     lo, hi = range(0, 4), range(4, 8)
+    half = 2 * POOL
     l_nw = done(Y.dma_start(T.nwt[:], T.nw[:]), 16)
     l_wr = lists(T.lwr, T.wr, 12, (("s", hi), ("y", lo)))
     l_wp = lists(T.lwp, T.wp, 12, (("s", hi), ("y", lo)))
     l_rd = lists(T.lrd, T.rd, 3, (("s", hi), ("y", lo)))
-    half = 2 * POOL
-    l_p0 = done(Y.dma_start(T.plt[:, 0:half], T.pl[:, 0:half]), 16)
-    l_p1 = done(S.dma_start(T.plt[:, half:2 * half], T.pl[:, half:2 * half]), 16)
-    l_qw = done(Y.dma_start(T.qwt[:], T.qw[:]), 16)
+    l_p = [done(S.dma_start(T.plt[:, 0:half], T.pl[:, 0:half]), 16)]
+    l_p.append(done(Y.dma_start(T.plt[:, half:2 * half], T.pl[:, half:2 * half]), 16))
     l_pg = lists(T.lpg, T.pg, 2, (("y", range(0, 8)),))
 
     i_p = done(g.iota(T.part[:], [[1, 1]], 0, 1))
     i_x = done(g.iota(T.xi[:], [[1, X4]], 0, 0, allow_small_or_imprecise_dtypes=True))
     i_c = done(g.iota(T.clb[:], [[16 * 16, 2]], 0, 0, allow_small_or_imprecise_dtypes=True))
-    i_k = done(g.iota(T.kt[:], [[16, 12]], WT + 1, 1))
+    i_k = done(g.iota(T.kt[:], [[16, 12]], WT, 1))
     i_v = done(g.iota(T.val[:], [[1, N * CW]], POOL, 0, allow_small_or_imprecise_dtypes=True))
 
     wait("v", i_p)
@@ -122,120 +129,115 @@ def rank_program(g, core, T, topo):
     wait("v", c_h)
     c_h16 = done(V.tensor_scalar(T.h16[:], T.ph[:], 16.0, None, A.mult))
     c_a = done(V.tensor_scalar(T.ca[:], T.ph[:], -64.0, 32.0, A.mult, A.add))
-    wait("v", c_h16, i_x)
-    c_w = [done(V.tensor_scalar(T.w[:, X4 * k:X4 * k + X4], T.xi[:], float(X4 * k), T.h16[:], A.add, A.subtract)) for k in range(4)]
-    wait("v", c_o, c_a)
-    c_b = done(V.tensor_scalar(T.cb[:], T.po[:], T.ca[:], T.h16[:], A.mult, A.add))
-    wait("v", c_b, c_i)
-    c_c = done(V.tensor_scalar(T.cc[:], T.pi[:], 16.0, T.cb[:], A.mult, A.add))
+    wait("v", c_i)
     c_f = done(V.tensor_copy(T.fi[:], T.pi[:]))
+    wait("v", c_o, c_h16, c_a)
+    c_b = done(V.tensor_scalar(T.cb[:], T.po[:], T.ca[:], T.h16[:], A.mult, A.add))
+    wait("v", i_x)
+    c_w = [done(V.tensor_scalar(T.w[:, X4 * k:X4 * k + X4], T.xi[:], float(X4 * k), T.h16[:], A.add, A.subtract)) for k in range(4)]
+    wait("v", c_b)
+    c_c = done(V.tensor_scalar(T.cc[:], T.pi[:], 16.0, T.cb[:], A.mult, A.add))
     wait("v", c_c, i_c)
     c_cl = done(V.tensor_scalar(T.clo[:], T.clb[:], T.cc[:], None, A.add))
 
-    wait("v", l_wr)
-    o_wr = done(V.tensor_scalar(T.wro[:], T.lwr[:], 0.0, None, A.max))
     wait("v", l_nw)
     q_nw = done(V.quantize_mx(T.nwc[:], T.nws[:], T.nwt[:]))
+    wait("v", l_wr)
+    o_wr = done(V.tensor_scalar(T.wro[:], T.lwr[:], 0.0, None, A.max))
+    wait("v", l_wp)
+    b_1 = done(V.tensor_scalar(T.ta[:], T.lwp[:], 1023, None, A.bitwise_and))
     wait("v", o_wr, q_nw)
-    a_c = done(V.tensor_copy(T.ac[:].bitcast(dt.uint32), T.nwc[:].bitcast(dt.uint32).indirect(T.wro[:])))
     wait("s", o_wr, q_nw)
-    a_s = done(S.activation(T.asc[:], T.nws[:].indirect(T.wro[:]), COPY))
-    o_own = done(V.tensor_scalar(T.owno[:, 0:3], T.lwr[:, 3 * rank:3 * rank + 3], 0.0, None, A.max))
-
-    wait("g", a_c, a_s)
     at = POOL + CW * rank
-    share = [(0, 4), (4, 6), (6, 8)], [(4, 8), (0, 2), (2, 4)]
-    cut = lambda t, i, w: t[:, w * i:w * i + w]
-    fused([(d, a, b, cut(T.ac, d, CW).bitcast(dt.uint8), T.wc[:, at:at + CW].bitcast(dt.uint8)) for d, (a, b) in zip(others, share[0])], "ra%d" % rank)
-    fused([(d, a, b, cut(T.asc, d, CW), T.wsc[:, at:at + CW]) for d, (a, b) in zip(others, share[1])], "ra%d" % rank)
+    first = lambda d: 3 * d // 2 * 2
+    wide = lambda d: 16 * (3 * d + 3 - first(d))
+    slots = lambda t, d: t[:, AW * d + wide(d) - CW:AW * d + wide(d)]
+    a_pick = {}
+    for d in others:
+        a, n = AW * d, wide(d)
+        a_pick["c", d] = done(V.tensor_copy(T.ac[:, a:a + n].bitcast(dt.uint32), T.nwc[:].bitcast(dt.uint32).indirect(T.wro[:, first(d):3 * d + 3])))
+        a_pick["s", d] = done(S.activation(T.asc[:, a:a + n], T.nws[:].indirect(T.wro[:, first(d):3 * d + 3]), COPY))
+    for kind, parts in A_CALLS:
+        wait("g", *[a_pick[kind, others[k]] for k, a, b in parts])
+        if kind == "c":
+            fused([(others[k], a, b, slots(T.ac, others[k]).bitcast(dt.uint8), T.wc[:, at:at + CW].bitcast(dt.uint8)) for k, a, b in parts], "ra%d" % rank)
+        else:
+            fused([(others[k], a, b, slots(T.asc, others[k]), T.wsc[:, at:at + CW]) for k, a, b in parts], "sa%d" % rank)
     i_s = done(g.iota(T.s16[:], [[16, N * CP]], 0, 0, allow_small_or_imprecise_dtypes=True))
 
-    def a_count(s):
-        o = sorted([d for d in range(N) if d != s], key=lambda d: -(0 if topo.mates(topo.chip(cores[s]), topo.chip(cores[d])) else 1 if topo.same_plane(topo.chip(cores[s]), topo.chip(cores[d])) else 2))
-        k = o.index(rank)
-        return sum(engines_in(*sh[k]) for sh in share)
+    hp = POOL // 2
 
-    wait("v", l_wp)
-    b_1 = done(V.tensor_scalar(T.ta[:], T.lwp[:], 0.0, None, A.is_lt))
+    def quantise(k):
+        wait("v", l_p[k])
+        return done(V.quantize_mx(T.wc[:, hp * k:hp * k + hp], T.wsc[:, hp * k:hp * k + hp], T.plt[:, half * k:half * k + half]))
+
     wait("v", i_k, b_1)
-    b_2 = done(V.tensor_tensor(T.tb[:], T.ta[:], T.kt[:], A.mult))
+    b_2 = done(V.tensor_tensor(T.tb[:], T.ta[:], T.kt[:], A.min))
+    o_own = done(V.tensor_scalar(T.owno[:, 0:3], T.lwr[:, 3 * rank:3 * rank + 3], 0.0, None, A.max))
     wait("v", b_2)
-    b_3 = done(V.tensor_tensor(T.tc[:], T.tb[:], T.lwp[:], A.add))
-    wait("v", b_3)
-    b_4 = done(V.tensor_scalar(T.wpo[:], T.tc[:], T.h16[:], None, A.add))
-    wait("v", l_rd)
-    b_5 = done(V.tensor_scalar(T.rdo[:, 0:3], T.lrd[:], 0.0, None, A.max))
-    wait("v", b_4, i_v, *c_w)
-    b_6 = done(V.tensor_copy(T.w[:].indirect(T.wpo[:]), T.val[:]))
+    b_4 = done(V.tensor_scalar(T.wpo[:], T.tb[:], T.h16[:], None, A.add))
     wait("v", o_own)
     n_c = done(V.tensor_copy(T.wc[:, at:at + CW].bitcast(dt.uint32), T.nwc[:].bitcast(dt.uint32).indirect(T.owno[:, 0:3])))
     wait("s", o_own)
     n_s = done(S.activation(T.wsc[:, at:at + CW], T.nws[:].indirect(T.owno[:, 0:3]), COPY))
+    wait("v", b_4, i_v, *c_w)
+    b_6 = done(V.tensor_copy(T.w[:].indirect(T.wpo[:]), T.val[:]))
+    q_0 = quantise(0)
     wait("v", b_6)
     b_7 = done(V.transpose(T.wt[:], T.w[:, 0:WT]))
+    q_1 = quantise(1)
     wait("v", b_7, c_cl)
     b_8 = done(V.tensor_copy(T.wm[:], T.wt[:].indirect(T.clo[:])))
+    wait("v", l_rd)
+    b_5 = done(V.tensor_scalar(T.rdo[:, 0:3], T.lrd[:], 0.0, None, A.max))
     wait("v", b_8, b_5)
     b_9 = done(V.tensor_copy(T.boff[:], T.wm[:].indirect(T.rdo[:, 0:3])))
-    hp = POOL // 2
-    wait("v", l_p0)
-    q_p0 = done(V.quantize_mx(T.wc[:, 0:hp], T.wsc[:, 0:hp], T.plt[:, 0:half]))
-    wait("v", l_p1)
-    q_p1 = done(V.quantize_mx(T.wc[:, hp:POOL], T.wsc[:, hp:POOL], T.plt[:, half:2 * half]))
-    wait("v", l_qw)
-    q_qw = done(V.quantize_mx(T.qwc[:], T.qws[:], T.qwt[:]))
 
-    arrived = [("ra%d" % s, a_count(s)) for s in others]
-    b_c, b_s = {}, {}
-    for q in ("v", "s"):
-        wait(q, b_9, q_p0, q_p1, n_c, n_s, *arrived)
+    arrived = [("ra%d" % s, count(A_CALLS, s, "c")) for s in others]
+    wait("v", b_9, q_0, q_1, n_c, *arrived)
+    wait("s", b_9, q_0, q_1, n_s, *[("sa%d" % s, count(A_CALLS, s, "s")) for s in others])
+    wait("y", arrived[0])
+    l_qw = done(Y.dma_start(T.qwt[:], T.qw[:]), 16)
+    cut = lambda t, i, w: t[:, w * i:w * i + w]
+    b_pick = {}
     for d in others + [rank]:
         c, s = (T.pc, T.psc) if d == rank else (T.bc, T.bsc)
-        b_c[d] = done(V.tensor_copy(cut(c, d, PC).bitcast(dt.uint32), T.wc[:].bitcast(dt.uint32).indirect(cut(T.boff, d, CP))))
-        b_s[d] = done(S.activation(cut(s, d, PC), T.wsc[:].indirect(cut(T.boff, d, CP)), COPY))
-    rb = "rb%d" % rank
-    codes = lambda d, a, b: (d, a, b, cut(T.bc, d, PC).bitcast(dt.uint8), cut(T.pc, rank, PC).bitcast(dt.uint8))
-    scales = lambda d, a, b: (d, a, b, cut(T.bsc, d, PC), cut(T.psc, rank, PC))
-    wait("g", b_c[others[0]])
-    fused([codes(others[0], 0, 8)], rb)
-    wait("g", b_c[others[1]])
-    fused([codes(others[1], 0, 8)], rb)
-    wait("g", b_s[others[0]], b_s[others[1]])
-    fused([scales(others[0], 0, 4), scales(others[1], 4, 8)], rb)
-    wait("g", b_c[others[2]])
-    fused([codes(others[2], 0, 8)], rb)
-    wait("g", b_s[others[2]])
-    fused([scales(others[2], 0, 8)], rb)
-
-    def b_count(s):
-        return engines_in(0, 8) + (engines_in(0, 8) if hops(s) == min(hops(d) for d in others) else engines_in(0, 4))
+        b_pick["c", d] = done(V.tensor_copy(cut(c, d, PC).bitcast(dt.uint32), T.wc[:].bitcast(dt.uint32).indirect(cut(T.boff, d, CP))))
+        b_pick["s", d] = done(S.activation(cut(s, d, PC), T.wsc[:].indirect(cut(T.boff, d, CP)), COPY))
+    for kind, parts in B_CALLS:
+        wait("g", *[b_pick[kind, others[k]] for k, a, b in parts])
+        if kind == "c":
+            fused([(others[k], a, b, cut(T.bc, others[k], PC).bitcast(dt.uint8), cut(T.pc, rank, PC).bitcast(dt.uint8)) for k, a, b in parts], "rb%d" % rank)
+        else:
+            fused([(others[k], a, b, cut(T.bsc, others[k], PC), cut(T.psc, rank, PC)) for k, a, b in parts], "rb%d" % rank)
 
     wait("v", l_pg, i_s, c_f)
     y_1 = done(V.tensor_copy(T.pgo[:], T.lpg[:]))
     y_2 = done(V.tensor_scalar(T.cw[:], T.s16[:], T.fi[:], None, A.add))
     wait("v", y_1, y_2)
     y_3 = done(V.tensor_copy(T.yoff[:], T.cw[:].indirect(T.pgo[:])))
+    wait("v", l_qw)
+    q_qw = done(V.quantize_mx(T.qwc[:], T.qws[:], T.qwt[:]))
 
     got = []
     for k, s in enumerate([rank] + others):
         if s == rank:
-            wait("t", q_qw, b_c[s], b_s[s])
+            wait("t", q_qw, b_pick["c", s], b_pick["s", s])
         else:
-            wait("t", ("rb%d" % s, b_count(s)))
+            wait("t", ("rb%d" % s, count(B_CALLS, s, "cs")))
         for o in range(O):
-            at = 512 * (O * k + o)
-            m = done(PE.matmul_mx(T.ps[:, at:at + PC], cut(T.qwc, o, 128), cut(T.qws, o, 128), cut(T.pc, s, PC), cut(T.psc, s, PC), True, True))
+            p = 512 * (O * k + o)
+            m = done(PE.matmul_mx(T.ps[:, p:p + PC], cut(T.qwc, o, 128), cut(T.qws, o, 128), cut(T.pc, s, PC), cut(T.psc, s, PC), True, True))
             if o == 0:
                 wait("v", m)
-                got.append(done(V.tensor_copy(cut(T.r0, s, PC), T.ps[:, at:at + PC])))
+                got.append(done(V.tensor_copy(cut(T.r0, s, PC), T.ps[:, p:p + PC])))
             else:
                 wait("s", m)
-                got.append(done(S.activation(cut(T.r1, s, PC), T.ps[:, at:at + PC], COPY)))
+                got.append(done(S.activation(cut(T.r1, s, PC), T.ps[:, p:p + PC], COPY)))
 
     wait("v", y_3, *got[0::2])
     wait("s", y_3, *got[1::2])
-    for k in range(2):
-        a, b = 256 * k, 256 * k + 256
+    for a, b in PIECES:
         f0 = done(V.tensor_copy(T.yt[:, a:b], T.r0[:].indirect(T.yoff[:, a // 16:b // 16])))
         f1 = done(S.activation(T.yt[:, 512 + a:512 + b], T.r1[:].indirect(T.yoff[:, a // 16:b // 16]), COPY))
         wait("y", f0)

from concourse.bass import DstId, RemoteDMATransfer
from concourse.mybir import dt, AluOpType, ActivationFunctionType

N = 4
PG, NW, SP, CW, CP, O = 32, 128, 32, 48, 12, 2
POOL = 16 * PG
WIN = POOL + N * CW
PC = 16 * CP
WT = POOL + 32
WALL = WT + 16 + N * CW + 112 + 16
X4 = WT // 4
AW = 64
X = "float8_e4m3fn_x4"

SCRATCH = {
    "nwt": ("sbuf", [128, 4 * NW], "bfloat16"), "plt": ("sbuf", [128, 4 * POOL], "bfloat16"), "qwt": ("sbuf", [128, 512 * O], "bfloat16"),
    "lwr": ("sbuf", [128, 12], "int32"), "lwp": ("sbuf", [128, 12], "int32"), "lrd": ("sbuf", [128, 3], "int32"), "lpg": ("sbuf", [128, 2], "int32"),
    "nwc": ("sbuf", [128, NW], X), "nws": ("sbuf", [128, NW], "uint8"),
    "ac": ("sbuf", [128, N * AW], X), "asc": ("sbuf", [128, N * AW], "uint8"),
    "wc": ("sbuf", [128, WIN], X), "wsc": ("sbuf", [128, WIN], "uint8"),
    "bc": ("sbuf", [128, N * PC], X), "bsc": ("sbuf", [128, N * PC], "uint8"),
    "pc": ("sbuf", [128, N * PC], X), "psc": ("sbuf", [128, N * PC], "uint8"),
    "qwc": ("sbuf", [128, 128 * O], X), "qws": ("sbuf", [128, 128 * O], "uint8"),
    "part": ("sbuf", [128, 1], "int32"), "pi": ("sbuf", [128, 1], "int32"), "ph": ("sbuf", [128, 1], "int32"), "po": ("sbuf", [128, 1], "int32"),
    "h16": ("sbuf", [128, 1], "float32"), "ca": ("sbuf", [128, 1], "float32"), "cb": ("sbuf", [128, 1], "float32"), "cc": ("sbuf", [128, 1], "float32"), "fi": ("sbuf", [128, 1], "float32"),
    "xi": ("sbuf", [128, X4], "float32"), "val": ("sbuf", [128, N * CW], "float32"), "kt": ("sbuf", [128, 12], "int32"),
    "clb": ("sbuf", [128, 2], "float32"), "s16": ("sbuf", [128, N * CP], "float32"), "cw": ("sbuf", [128, N * CP], "float32"),
    "clo": ("sbuf", [128, 2], "uint16"), "wro": ("sbuf", [128, 12], "uint16"), "owno": ("sbuf", [128, 4], "uint16"),
    "wpo": ("sbuf", [128, 12], "uint16"), "rdo": ("sbuf", [128, 4], "uint16"), "pgo": ("sbuf", [128, 2], "uint16"),
    "boff": ("sbuf", [128, N * CP], "uint16"), "yoff": ("sbuf", [128, SP], "uint16"),
    "ta": ("sbuf", [128, 12], "int32"), "tb": ("sbuf", [128, 12], "int32"),
    "w": ("sbuf", [128, WALL], "float32"), "wt": ("sbuf", [128, WT], "float32"), "wm": ("sbuf", [128, PG], "float32"),
    "r0": ("sbuf", [128, N * PC], "float32"), "r1": ("sbuf", [128, N * PC], "float32"),
    "yt": ("sbuf", [128, 512 * O], "float32"),
    "ps": ("psum", [128, 512 * 2 * N], "float32"),
}
TOK = 110
SEMAPHORES = ["t%d" % i for i in range(TOK)] + [p + "%d" % i for p in ("ra", "sa", "rb") for i in range(N)] + ["left"]

A_CALLS = [("c", [(0, 0, 4)]), ("c", [(1, 4, 6), (2, 6, 8)]), ("s", [(0, 4, 8), (1, 0, 2), (2, 2, 4)])]
B_CALLS = [("c", [(0, 0, 8)]), ("c", [(1, 0, 8)]), ("s", [(0, 0, 4), (1, 4, 8)]), ("c", [(2, 0, 8)]), ("s", [(2, 0, 8)])]
PIECES = [(0, 192), (192, 512)]


def rank_program(g, core, T, topo):
    rank = T.rank_of(core)
    if rank is None:
        return
    V, S, Y, PE = g.vector, g.scalar, g.sync, g.tensor
    A, COPY = AluOpType, ActivationFunctionType.Copy
    cores = list(T.cores)

    used, seen, toks = [0], set(), []
    queues = {"g": g, "v": V, "s": S, "y": Y, "t": PE}

    def tok():
        k = "t%d" % used[0]
        used[0] += 1
        return k

    def done(ins, n=1):
        k = tok()
        ins.then_inc(T.sem[k], n)
        toks.append((k, n))
        return (k, n)

    def wait(q, *ts):
        for t in ts:
            if (q, t) not in seen:
                seen.add((q, t))
                queues[q].wait_ge(T.sem[t[0]], t[1])

    def hops(s, d):
        a, b = topo.chip(cores[s]), topo.chip(cores[d])
        return 0 if topo.mates(a, b) else 1 if topo.same_plane(a, b) else 2

    def away(s):
        return sorted([d for d in range(N) if d != s], key=lambda d: -hops(s, d))

    others = away(rank)

    def engines(d, a, b):
        e = topo.engines(core, cores[d])
        return e[a * len(e) // 8:b * len(e) // 8]

    left = [0]

    def fused(parts, sem):
        ts = []
        for d, a, b, src, dst in parts:
            rid, pid, _ = topo.addr(cores[d])
            e = engines(d, a, b)
            ts.append(RemoteDMATransfer(dst_ids=[DstId(rid=rid, pnc=pid)], dma_engine_mask=sum(1 << k for k in e), remote_sem=T.sem[sem], src=src, dst=dst))
            left[0] += len(e)
        g.remote_dma_fused(ts, local_sem=T.sem.left)

    def count(calls, s, kinds):
        n = len(topo.engines(cores[s], core))
        return sum(b * n // 8 - a * n // 8 for kind, parts in calls for k, a, b in parts if kind in kinds and away(s)[k] == rank)

    def lists(dst, src, n, halves):
        k = tok()
        for q, gr in halves:
            for i in gr:
                queues[q].dma_start(dst[16 * i:16 * i + 16, 0:n], src[:]).then_inc(T.sem[k], 16)
        toks.append((k, 128))
        return (k, 128)

    lo, hi = range(0, 4), range(4, 8)
    half = 2 * POOL
    l_nw = done(Y.dma_start(T.nwt[:], T.nw[:]), 16)
    l_wr = lists(T.lwr, T.wr, 12, (("s", hi), ("y", lo)))
    l_wp = lists(T.lwp, T.wp, 12, (("s", hi), ("y", lo)))
    l_rd = lists(T.lrd, T.rd, 3, (("s", hi), ("y", lo)))
    l_p = [done(S.dma_start(T.plt[:, 0:half], T.pl[:, 0:half]), 16)]
    l_p.append(done(Y.dma_start(T.plt[:, half:2 * half], T.pl[:, half:2 * half]), 16))
    l_pg = lists(T.lpg, T.pg, 2, (("y", range(0, 8)),))

    i_p = done(g.iota(T.part[:], [[1, 1]], 0, 1))
    i_x = done(g.iota(T.xi[:], [[1, X4]], 0, 0, allow_small_or_imprecise_dtypes=True))
    i_c = done(g.iota(T.clb[:], [[16 * 16, 2]], 0, 0, allow_small_or_imprecise_dtypes=True))
    i_k = done(g.iota(T.kt[:], [[16, 12]], WT, 1))
    i_v = done(g.iota(T.val[:], [[1, N * CW]], POOL, 0, allow_small_or_imprecise_dtypes=True))

    wait("v", i_p)
    c_h = done(V.tensor_scalar(T.ph[:], T.part[:], 4, 1, A.logical_shift_right, A.bitwise_and))
    c_i = done(V.tensor_scalar(T.pi[:], T.part[:], 15, None, A.bitwise_and))
    c_o = done(V.tensor_scalar(T.po[:], T.part[:], 1, None, A.bitwise_and))
    wait("v", c_h)
    c_h16 = done(V.tensor_scalar(T.h16[:], T.ph[:], 16.0, None, A.mult))
    c_a = done(V.tensor_scalar(T.ca[:], T.ph[:], -64.0, 32.0, A.mult, A.add))
    wait("v", c_i)
    c_f = done(V.tensor_copy(T.fi[:], T.pi[:]))
    wait("v", c_o, c_h16, c_a)
    c_b = done(V.tensor_scalar(T.cb[:], T.po[:], T.ca[:], T.h16[:], A.mult, A.add))
    wait("v", i_x)
    c_w = [done(V.tensor_scalar(T.w[:, X4 * k:X4 * k + X4], T.xi[:], float(X4 * k), T.h16[:], A.add, A.subtract)) for k in range(4)]
    wait("v", c_b)
    c_c = done(V.tensor_scalar(T.cc[:], T.pi[:], 16.0, T.cb[:], A.mult, A.add))
    wait("v", c_c, i_c)
    c_cl = done(V.tensor_scalar(T.clo[:], T.clb[:], T.cc[:], None, A.add))

    wait("v", l_nw)
    q_nw = done(V.quantize_mx(T.nwc[:], T.nws[:], T.nwt[:]))
    wait("v", l_wr)
    o_wr = done(V.tensor_scalar(T.wro[:], T.lwr[:], 0.0, None, A.max))
    wait("v", l_wp)
    b_1 = done(V.tensor_scalar(T.ta[:], T.lwp[:], 1023, None, A.bitwise_and))
    wait("v", o_wr, q_nw)
    wait("s", o_wr, q_nw)
    at = POOL + CW * rank
    first = lambda d: 3 * d // 2 * 2
    wide = lambda d: 16 * (3 * d + 3 - first(d))
    slots = lambda t, d: t[:, AW * d + wide(d) - CW:AW * d + wide(d)]
    a_pick = {}
    for d in others:
        a, n = AW * d, wide(d)
        a_pick["c", d] = done(V.tensor_copy(T.ac[:, a:a + n].bitcast(dt.uint32), T.nwc[:].bitcast(dt.uint32).indirect(T.wro[:, first(d):3 * d + 3])))
        a_pick["s", d] = done(S.activation(T.asc[:, a:a + n], T.nws[:].indirect(T.wro[:, first(d):3 * d + 3]), COPY))
    for kind, parts in A_CALLS:
        wait("g", *[a_pick[kind, others[k]] for k, a, b in parts])
        if kind == "c":
            fused([(others[k], a, b, slots(T.ac, others[k]).bitcast(dt.uint8), T.wc[:, at:at + CW].bitcast(dt.uint8)) for k, a, b in parts], "ra%d" % rank)
        else:
            fused([(others[k], a, b, slots(T.asc, others[k]), T.wsc[:, at:at + CW]) for k, a, b in parts], "sa%d" % rank)
    i_s = done(g.iota(T.s16[:], [[16, N * CP]], 0, 0, allow_small_or_imprecise_dtypes=True))

    hp = POOL // 2

    def quantise(k):
        wait("v", l_p[k])
        return done(V.quantize_mx(T.wc[:, hp * k:hp * k + hp], T.wsc[:, hp * k:hp * k + hp], T.plt[:, half * k:half * k + half]))

    wait("v", i_k, b_1)
    b_2 = done(V.tensor_tensor(T.tb[:], T.ta[:], T.kt[:], A.min))
    o_own = done(V.tensor_scalar(T.owno[:, 0:3], T.lwr[:, 3 * rank:3 * rank + 3], 0.0, None, A.max))
    wait("v", b_2)
    b_4 = done(V.tensor_scalar(T.wpo[:], T.tb[:], T.h16[:], None, A.add))
    wait("v", o_own)
    n_c = done(V.tensor_copy(T.wc[:, at:at + CW].bitcast(dt.uint32), T.nwc[:].bitcast(dt.uint32).indirect(T.owno[:, 0:3])))
    wait("s", o_own)
    n_s = done(S.activation(T.wsc[:, at:at + CW], T.nws[:].indirect(T.owno[:, 0:3]), COPY))
    wait("v", b_4, i_v, *c_w)
    b_6 = done(V.tensor_copy(T.w[:].indirect(T.wpo[:]), T.val[:]))
    q_0 = quantise(0)
    wait("v", b_6)
    b_7 = done(V.transpose(T.wt[:], T.w[:, 0:WT]))
    q_1 = quantise(1)
    wait("v", b_7, c_cl)
    b_8 = done(V.tensor_copy(T.wm[:], T.wt[:].indirect(T.clo[:])))
    wait("v", l_rd)
    b_5 = done(V.tensor_scalar(T.rdo[:, 0:3], T.lrd[:], 0.0, None, A.max))
    wait("v", b_8, b_5)
    b_9 = done(V.tensor_copy(T.boff[:], T.wm[:].indirect(T.rdo[:, 0:3])))

    arrived = [("ra%d" % s, count(A_CALLS, s, "c")) for s in others]
    wait("v", b_9, q_0, q_1, n_c, *arrived)
    wait("s", b_9, q_0, q_1, n_s, *[("sa%d" % s, count(A_CALLS, s, "s")) for s in others])
    wait("y", arrived[0])
    l_qw = done(Y.dma_start(T.qwt[:], T.qw[:]), 16)
    cut = lambda t, i, w: t[:, w * i:w * i + w]
    b_pick = {}
    for d in others + [rank]:
        c, s = (T.pc, T.psc) if d == rank else (T.bc, T.bsc)
        b_pick["c", d] = done(V.tensor_copy(cut(c, d, PC).bitcast(dt.uint32), T.wc[:].bitcast(dt.uint32).indirect(cut(T.boff, d, CP))))
        b_pick["s", d] = done(S.activation(cut(s, d, PC), T.wsc[:].indirect(cut(T.boff, d, CP)), COPY))
    for kind, parts in B_CALLS:
        wait("g", *[b_pick[kind, others[k]] for k, a, b in parts])
        if kind == "c":
            fused([(others[k], a, b, cut(T.bc, others[k], PC).bitcast(dt.uint8), cut(T.pc, rank, PC).bitcast(dt.uint8)) for k, a, b in parts], "rb%d" % rank)
        else:
            fused([(others[k], a, b, cut(T.bsc, others[k], PC), cut(T.psc, rank, PC)) for k, a, b in parts], "rb%d" % rank)

    wait("v", l_pg, i_s, c_f)
    y_1 = done(V.tensor_copy(T.pgo[:], T.lpg[:]))
    y_2 = done(V.tensor_scalar(T.cw[:], T.s16[:], T.fi[:], None, A.add))
    wait("v", y_1, y_2)
    y_3 = done(V.tensor_copy(T.yoff[:], T.cw[:].indirect(T.pgo[:])))
    wait("v", l_qw)
    q_qw = done(V.quantize_mx(T.qwc[:], T.qws[:], T.qwt[:]))

    got = []
    for k, s in enumerate([rank] + others):
        if s == rank:
            wait("t", q_qw, b_pick["c", s], b_pick["s", s])
        else:
            wait("t", ("rb%d" % s, count(B_CALLS, s, "cs")))
        for o in range(O):
            p = 512 * (O * k + o)
            m = done(PE.matmul_mx(T.ps[:, p:p + PC], cut(T.qwc, o, 128), cut(T.qws, o, 128), cut(T.pc, s, PC), cut(T.psc, s, PC), True, True))
            if o == 0:
                wait("v", m)
                got.append(done(V.tensor_copy(cut(T.r0, s, PC), T.ps[:, p:p + PC])))
            else:
                wait("s", m)
                got.append(done(S.activation(cut(T.r1, s, PC), T.ps[:, p:p + PC], COPY)))

    wait("v", y_3, *got[0::2])
    wait("s", y_3, *got[1::2])
    for a, b in PIECES:
        f0 = done(V.tensor_copy(T.yt[:, a:b], T.r0[:].indirect(T.yoff[:, a // 16:b // 16])))
        f1 = done(S.activation(T.yt[:, 512 + a:512 + b], T.r1[:].indirect(T.yoff[:, a // 16:b // 16]), COPY))
        wait("y", f0)
        done(Y.dma_start(T.y[:, a:b], T.yt[:, a:b]), 16)
        wait("y", f1)
        done(Y.dma_start(T.y[:, 512 + a:512 + b], T.yt[:, 512 + a:512 + b]), 16)

    for t in toks:
        if not any((q, t) in seen for q in queues):
            wait("y", t)
    g.wait_ge(T.sem.left, left[0])
